import numpy as np
CORES = [18,22,26,30,146,150,154,158]
N = 8
DEAD = {"mate_links":[[2,0],[2,1]],"switch_ports":[[19,0]],"chips":[]}
def setup_inputs(rng):
    return {"x": rng.standard_normal((N, 128, 256), dtype=np.float32)}
def reference(x):
    g = np.concatenate(list(x), axis=1)
    return {"y": np.broadcast_to(g, (N,) + g.shape)}

@@ -1,0 +1,268 @@
+from concourse.bass import DstId, RemoteDMATransfer
+
+SCRATCH = {"buf": ("dram", [16, 128, 128], "float32")}
+SEMAPHORES = ["ld", "st", "snt", "sn0"] + ["p%d" % h for h in range(16)]
+
+CFG = {
+    "hop1": "LH",
+    "D_a": "DD",
+    "B_a": "SDh", "B_a_side": [[1, 1], [1, 1]],
+    "B_c1": ("peer", "SDh"), "B_d1": ("help", "SDh"),
+    "A_b": "DD", "C_b": "DD", "b_side": [[1, 1], [0, 0]],
+    "D_b1": ("relay", "DD"),
+    "merge": False, "own": "sent", "split": 0,
+}
+
+
+def wc(host, chip, c):
+    return 128 * host + 8 * chip + c
+
+
+def build(cores, cfg):
+    A, B, C, D = (tuple(cores[0:2]), tuple(cores[2:4]), tuple(cores[4:6]), tuple(cores[6:8]))
+    kids = {}
+    pairs = [(h, p) for p in (2, 3, 4, 5, 6, 7, 0) for h in (0, 1)]
+    used = [0]
+
+    def relay(parity, side):
+        h, p = pairs[used[0]]
+        used[0] += 1
+        return wc(h, 2 * p + parity, 2 + 4 * side)
+
+    def edge(h, s, t):
+        kids.setdefault((s, h), []).append(t)
+
+    lh = {}
+    free = {}
+
+    def helper(X, h, s):
+        key = (X[0], h // 2)
+        if key not in lh:
+            side = (s % 8) // 4
+            lst = free.setdefault((X[0], side), [1, -1, -2])
+            if not lst:
+                lst = free.setdefault((X[0], 1 - side), [1, -1, -2])
+                side = 1 - side
+            lh[key] = X[side] + lst.pop(0)
+        return lh[key]
+
+    def deliver(h, s, X, pol):
+        if pol == "DD":
+            edge(h, s, X[0])
+            edge(h, s, X[1])
+            return None
+        if pol == "LH":
+            r = helper(X, h, s)
+            edge(h, s, r)
+            edge(h, r, X[0])
+            edge(h, r, X[1])
+            return r
+        f = (h % 2) if pol == "SDh" else int(pol[2])
+        edge(h, s, X[f])
+        edge(h, X[f], X[1 - f])
+        return X[f]
+
+    def pol1(i):
+        return {"h": "SDh", "LH": "LH"}.get(cfg["hop1"], "SD%d" % i)
+
+    def polr(pol, side):
+        return ("SD%d" % side) if pol == "SD" else pol
+
+    for i in (0, 1):
+        for k in (0, 1):
+            h = 2 * i + k
+            edge(h, A[i], A[1 - i])
+            f = deliver(h, A[i], C, pol1(i))
+            deliver(h, f, D, polr(cfg["D_a"], (f % 8) // 4))
+            sd = cfg["B_a_side"][i][k]
+            r = relay(0, sd)
+            edge(h, A[i], r)
+            deliver(h, r, B, polr(cfg["B_a"], sd))
+            h = 4 + 2 * i + k
+            edge(h, B[i], B[1 - i])
+            sd = cfg["b_side"][i][k]
+            r = relay(1, sd)
+            edge(h, B[i], r)
+            deliver(h, r, A, polr(cfg["A_b"], sd))
+            deliver(h, r, C, polr(cfg["C_b"], sd))
+            if i == 0:
+                deliver(h, B[0], D, pol1(0))
+            else:
+                kind, pol = cfg["D_b1"]
+                if kind == "peer":
+                    deliver(h, B[0], D, polr(pol, 0))
+                elif kind == "help":
+                    edge(h, B[1], B[0] + 1)
+                    deliver(h, B[0] + 1, D, polr(pol, 0))
+                else:
+                    deliver(h, r, D, polr(pol, 0))
+            for (X, O, base, key) in ((C, D, 8, "B_c1"), (D, C, 12, "B_d1")):
+                h = base + 2 * i + k
+                edge(h, X[i], X[1 - i])
+                deliver(h, X[i], A, pol1(i))
+                deliver(h, X[i], O, pol1(i))
+                if i == 0:
+                    deliver(h, X[0], B, pol1(0))
+                else:
+                    kind, pol = cfg[key]
+                    if kind == "peer":
+                        deliver(h, X[0], B, polr(pol, 0))
+                    elif kind == "help":
+                        r = X[0] + 1 if X is C else helper(X, h, X[0])
+                        edge(h, X[1], r)
+                        deliver(h, r, B, polr(pol, 0))
+                    else:
+                        r = relay(0, 1)
+                        edge(h, X[1], r)
+                        deliver(h, r, B, polr(pol, 1))
+
+    est = {}
+
+    def walk(h, s, t0):
+        for t in kids.get((s, h), []):
+            est[(t, h)] = t0 + (1.0 if t // 8 == s // 8 else 1.5)
+            walk(h, t, est[(t, h)])
+
+    for h in range(16):
+        est[(cores[h // 2], h)] = 0.0
+        walk(h, cores[h // 2], 0.0)
+
+    cnt = {}
+
+    def alloc(s, tasks):
+        off, on, trs = [], [], []
+        for (h, ds) in tasks:
+            o = [t for t in ds if t // 8 != s // 8]
+            n = [t for t in ds if t // 8 == s // 8]
+            if o:
+                off.append((h, o))
+            if n:
+                on.append((h, n))
+
+        def place(lst, base, width):
+            n = 1
+            while n < len(lst):
+                n *= 2
+            e = width // n
+            for q, (h, ds) in enumerate(lst):
+                trs.append((h, ds, ((1 << e) - 1) << (base + q * e), e))
+                for t in ds:
+                    cnt[(t, h)] = e
+
+        if off and on:
+            place(off, 0, 8)
+            place(on, 8, 8)
+        elif off:
+            place(off, 0, 8)
+        else:
+            place(on, 0, 16)
+        return trs
+
+    def height(t, h):
+        return max([0.0] + [(1.0 if u // 8 == t // 8 else 1.5) + height(u, h) for u in kids.get((t, h), [])])
+
+    senders = sorted(set(s for (s, h) in kids))
+    calls = {}
+    for s in senders:
+        groups = {}
+        for (s2, h) in sorted(kids):
+            if s2 == s:
+                e = est[(s, h)]
+                if e == 0.0 and cfg.get("split"):
+                    urgent = [t for t in kids[(s, h)] if height(t, h) >= cfg["split"]]
+                    late = [t for t in kids[(s, h)] if t not in urgent]
+                    if urgent:
+                        groups.setdefault((e, 0), []).append((h, urgent))
+                    if late:
+                        groups.setdefault((e, 1), []).append((h, late))
+                else:
+                    groups.setdefault((e, 0 if (cfg["merge"] or e == 0.0) else h // 2), []).append((h, kids[(s, h)]))
+        calls[s] = [(key, sorted(set(h for (h, _d) in groups[key])), alloc(s, groups[key])) for key in sorted(groups)]
+
+    prog = {}
+    for s in senders:
+        gq, sy, sc = [], [], []
+        total = 0
+        n0 = 0
+        rank = cores.index(s) if s in cores else None
+        for (key, hs, trs) in calls[s]:
+            n = sum(e for (_h, _d, _m, e) in trs)
+            if key[0] == 0.0:
+                if not sy:
+                    sy.append(("load", rank))
+                    gq.append(("wait", "ld", 16))
+                gq.append(("send", trs, "sn0"))
+                n0 += n
+            else:
+                for h in hs:
+                    gq.append(("wait", "p%d" % h, cnt[(s, h)]))
+                gq.append(("send", trs, "snt"))
+                total += n
+        if rank is not None:
+            if cfg["own"] == "sent":
+                sc.append(("wait", "sn0", n0))
+            else:
+                gq.append(("wait", "sn0", n0))
+                if cfg["own"] == "ld":
+                    sc.append(("wait", "ld", 16))
+            sc.append(("own", rank))
+            items = []
+            for j in range(8):
+                if j == rank:
+                    continue
+                e0, e1 = est[(s, 2 * j)], est[(s, 2 * j + 1)]
+                if e0 == e1:
+                    items.append((e0, j, None))
+                else:
+                    items.append((e0, j, 0))
+                    items.append((e1, j, 1))
+            items.sort(key=lambda it: (it[0], it[1]))
+            for q, (e, j, k) in enumerate(items):
+                dq = sy if q % 2 == 0 else sc
+                for h in ((2 * j, 2 * j + 1) if k is None else (2 * j + k,)):
+                    dq.append(("wait", "p%d" % h, cnt[(s, h)]))
+                dq.append(("store", j, k))
+            if total:
+                gq.append(("wait", "snt", total))
+            gq.append(("wait", "st", 16 * (len(items) + 1)))
+        else:
+            gq.append(("wait", "snt", total))
+        prog[s] = {"g": gq, "sync": sy, "scalar": sc}
+    return prog
+
+
+CACHE = {}
+
+
+def rank_program(g, core, T, topo):
+    if "p" not in CACHE:
+        CACHE["p"] = build(list(T.cores), CFG)
+    prog = CACHE["p"].get(core)
+    if prog is None:
+        return
+    for name, q in (("sync", g.sync), ("scalar", g.scalar), ("g", g)):
+        for op in prog[name]:
+            if op[0] == "wait":
+                q.wait_ge(T.sem[op[1]], op[2])
+            elif op[0] == "load":
+                r = op[1]
+                q.dma_start(T.buf[2 * r:2 * r + 2], T.x[:]).then_inc(T.sem.ld, 16)
+            elif op[0] == "own":
+                r = op[1]
+                q.dma_start(T.y[:, 256 * r:256 * r + 256], T.x[:]).then_inc(T.sem.st, 16)
+            elif op[0] == "store":
+                j, k = op[1], op[2]
+                if k is None:
+                    q.dma_start(T.y[:, 256 * j:256 * j + 256], T.buf[2 * j:2 * j + 2]).then_inc(T.sem.st, 16)
+                else:
+                    q.dma_start(T.y[64 * k:64 * k + 64, 256 * j:256 * j + 256], T.buf[2 * j + k]).then_inc(T.sem.st, 16)
+            else:
+                trs = []
+                for (h, ds, mask, _e) in op[1]:
+                    ids = []
+                    for t in ds:
+                        rid, pid = topo.addr(t, core)
+                        ids.append(DstId(rid=rid, pnc=pid))
+                    trs.append(RemoteDMATransfer(dst_ids=ids, dma_engine_mask=mask, remote_sem=T.sem["p%d" % h],
+                                                 srcs=[T.buf[h]], dsts=[T.buf[h] for _t in ds]))
+                q.remote_dma_fused(trs, local_sem=T.sem[op[2]])

@@ -4,13 +4,13 @@ SCRATCH = {"buf": ("dram", [16, 128, 128], "float32")}
 SEMAPHORES = ["ld", "st", "snt", "sn0"] + ["p%d" % h for h in range(16)]
 
 CFG = {
-    "hop1": "LH",
+    "hop1": {"A": "LH", "B": "LH", "C": "LH", "D": "LH"},
     "D_a": "DD",
     "B_a": "SDh", "B_a_side": [[1, 1], [1, 1]],
     "B_c1": ("peer", "SDh"), "B_d1": ("help", "SDh"),
     "A_b": "DD", "C_b": "DD", "b_side": [[1, 1], [0, 0]],
     "D_b1": ("relay", "DD"),
-    "merge": False, "own": "sent", "split": 0,
+    "merge": True, "own": "sent", "split": 0, "order": True,
 }
 
 
@@ -20,6 +20,7 @@ def wc(host, chip, c):
 
 def build(cores, cfg):
     A, B, C, D = (tuple(cores[0:2]), tuple(cores[2:4]), tuple(cores[4:6]), tuple(cores[6:8]))
+    names = {A: "A", B: "B", C: "C", D: "D"}
     kids = {}
     pairs = [(h, p) for p in (2, 3, 4, 5, 6, 7, 0) for h in (0, 1)]
     used = [0]
@@ -62,8 +63,8 @@ def build(cores, cfg):
         edge(h, X[f], X[1 - f])
         return X[f]
 
-    def pol1(i):
-        return {"h": "SDh", "LH": "LH"}.get(cfg["hop1"], "SD%d" % i)
+    def pol1(i, X):
+        return {"h": "SDh", "LH": "LH", "DD": "DD"}.get(cfg["hop1"][names[X]], "SD%d" % i)
 
     def polr(pol, side):
         return ("SD%d" % side) if pol == "SD" else pol
@@ -72,7 +73,7 @@ def build(cores, cfg):
         for k in (0, 1):
             h = 2 * i + k
             edge(h, A[i], A[1 - i])
-            f = deliver(h, A[i], C, pol1(i))
+            f = deliver(h, A[i], C, pol1(i, C))
             deliver(h, f, D, polr(cfg["D_a"], (f % 8) // 4))
             sd = cfg["B_a_side"][i][k]
             r = relay(0, sd)
@@ -86,7 +87,7 @@ def build(cores, cfg):
             deliver(h, r, A, polr(cfg["A_b"], sd))
             deliver(h, r, C, polr(cfg["C_b"], sd))
             if i == 0:
-                deliver(h, B[0], D, pol1(0))
+                deliver(h, B[0], D, pol1(0, D))
             else:
                 kind, pol = cfg["D_b1"]
                 if kind == "peer":
@@ -99,10 +100,10 @@ def build(cores, cfg):
             for (X, O, base, key) in ((C, D, 8, "B_c1"), (D, C, 12, "B_d1")):
                 h = base + 2 * i + k
                 edge(h, X[i], X[1 - i])
-                deliver(h, X[i], A, pol1(i))
-                deliver(h, X[i], O, pol1(i))
+                deliver(h, X[i], A, pol1(i, A))
+                deliver(h, X[i], O, pol1(i, O))
                 if i == 0:
-                    deliver(h, X[0], B, pol1(0))
+                    deliver(h, X[0], B, pol1(0, B))
                 else:
                     kind, pol = cfg[key]
                     if kind == "peer":
@@ -127,11 +128,15 @@ def build(cores, cfg):
         est[(cores[h // 2], h)] = 0.0
         walk(h, cores[h // 2], 0.0)
 
+    def height(t, h):
+        return max([0.0] + [(1.0 if u // 8 == t // 8 else 1.5) + height(u, h) for u in kids.get((t, h), [])])
+
     cnt = {}
 
     def alloc(s, tasks):
         off, on, trs = [], [], []
-        for (h, ds) in tasks:
+        for (h, ds0) in tasks:
+            ds = sorted(ds0, key=lambda t: -height(t, h)) if cfg["order"] else ds0
             o = [t for t in ds if t // 8 != s // 8]
             n = [t for t in ds if t // 8 == s // 8]
             if o:
@@ -158,9 +163,6 @@ def build(cores, cfg):
             place(on, 0, 16)
         return trs
 
-    def height(t, h):
-        return max([0.0] + [(1.0 if u // 8 == t // 8 else 1.5) + height(u, h) for u in kids.get((t, h), [])])
-
     senders = sorted(set(s for (s, h) in kids))
     calls = {}
     for s in senders:
@@ -168,13 +170,15 @@ def build(cores, cfg):
         for (s2, h) in sorted(kids):
             if s2 == s:
                 e = est[(s, h)]
-                if e == 0.0 and cfg.get("split"):
+                if e == 0.0 and cfg["split"]:
                     urgent = [t for t in kids[(s, h)] if height(t, h) >= cfg["split"]]
                     late = [t for t in kids[(s, h)] if t not in urgent]
                     if urgent:
                         groups.setdefault((e, 0), []).append((h, urgent))
                     if late:
                         groups.setdefault((e, 1), []).append((h, late))
+                elif cfg["merge"] == "all" and e >= 2.5:
+                    groups.setdefault((9.0, 0), []).append((h, kids[(s, h)]))
                 else:
                     groups.setdefault((e, 0 if (cfg["merge"] or e == 0.0) else h // 2), []).append((h, kids[(s, h)]))
         calls[s] = [(key, sorted(set(h for (h, _d) in groups[key])), alloc(s, groups[key])) for key in sorted(groups)]

@@ -7,9 +7,9 @@ CFG = {
     "hop1": {"A": "LH", "B": "LH", "C": "LH", "D": "LH"},
     "D_a": "DD",
     "B_a": "SDh", "B_a_side": [[1, 1], [1, 1]],
-    "B_c1": ("peer", "SDh"), "B_d1": ("help", "SDh"),
+    "B_c1": ("help", "SDh"), "B_d1": ("help", "SDh"),
     "A_b": "DD", "C_b": "DD", "b_side": [[1, 1], [0, 0]],
-    "D_b1": ("relay", "DD"),
+    "D_b1": ("help", "DD"), "C_a": "four", "lh_half": "B",
     "merge": True, "own": "sent", "split": 0, "order": True,
 }
 
@@ -36,8 +36,12 @@ def build(cores, cfg):
     lh = {}
     free = {}
 
+    if cfg["C_a"] == "four":
+        free[(C[0], 0)] = [-1, -2]
+        free[(C[0], 1)] = [-1, -2]
+
     def helper(X, h, s):
-        key = (X[0], h // 2)
+        key = (X[0], h if names[X] in cfg["lh_half"] else 100 + h // 2)
         if key not in lh:
             side = (s % 8) // 4
             lst = free.setdefault((X[0], side), [1, -1, -2])
@@ -73,8 +77,15 @@ def build(cores, cfg):
         for k in (0, 1):
             h = 2 * i + k
             edge(h, A[i], A[1 - i])
-            f = deliver(h, A[i], C, pol1(i, C))
-            deliver(h, f, D, polr(cfg["D_a"], (f % 8) // 4))
+            if cfg["C_a"] == "four":
+                f = C[i] + (1 if k != i else 0)
+                edge(h, A[i], f)
+                for t in (D[0], D[1], C[0], C[1]):
+                    if t != f:
+                        edge(h, f, t)
+            else:
+                f = deliver(h, A[i], C, pol1(i, C))
+                deliver(h, f, D, polr(cfg["D_a"], (f % 8) // 4))
             sd = cfg["B_a_side"][i][k]
             r = relay(0, sd)
             edge(h, A[i], r)

@@ -7,7 +7,7 @@ CFG = {
     "hop1": {"A": "LH", "B": "LH", "C": "LH", "D": "LH"},
     "D_a": "DD",
     "B_a": "SDh", "B_a_side": [[1, 1], [1, 1]],
-    "B_c1": ("help", "SDh"), "B_d1": ("help", "SDh"),
+    "B_c1": ("via", "SDh"), "B_d1": ("help", "SDh"),
     "A_b": "DD", "C_b": "DD", "b_side": [[1, 1], [0, 0]],
     "D_b1": ("help", "DD"), "C_a": "four", "lh_half": "B",
     "merge": True, "own": "sent", "split": 0, "order": True,
@@ -112,6 +112,13 @@ def build(cores, cfg):
                 h = base + 2 * i + k
                 edge(h, X[i], X[1 - i])
                 deliver(h, X[i], A, pol1(i, A))
+                if i == 1 and cfg[key][0] == "via":
+                    r = helper(D, 14, D[0])
+                    edge(h, X[1], r)
+                    edge(h, r, D[0])
+                    edge(h, r, D[1])
+                    deliver(h, r, B, polr(cfg[key][1], 0))
+                    continue
                 deliver(h, X[i], O, pol1(i, O))
                 if i == 0:
                     deliver(h, X[0], B, pol1(0, B))

from concourse.bass import DstId, RemoteDMATransfer

SCRATCH = {"buf": ("dram", [16, 128, 128], "float32")}
SEMAPHORES = ["ld", "st", "snt", "sn0"] + ["p%d" % h for h in range(16)]

CFG = {
    "hop1": {"A": "LH", "B": "LH", "C": "LH", "D": "LH"},
    "D_a": "DD",
    "B_a": "SDh", "B_a_side": [[1, 1], [1, 1]],
    "B_c1": ("via", "SDh"), "B_d1": ("help", "SDh"),
    "A_b": "DD", "C_b": "DD", "b_side": [[1, 1], [0, 0]],
    "D_b1": ("help", "DD"), "C_a": "four", "lh_half": "B",
    "merge": True, "own": "sent", "split": 0, "order": True,
}


def wc(host, chip, c):
    return 128 * host + 8 * chip + c


def build(cores, cfg):
    A, B, C, D = (tuple(cores[0:2]), tuple(cores[2:4]), tuple(cores[4:6]), tuple(cores[6:8]))
    names = {A: "A", B: "B", C: "C", D: "D"}
    kids = {}
    pairs = [(h, p) for p in (2, 3, 4, 5, 6, 7, 0) for h in (0, 1)]
    used = [0]

    def relay(parity, side):
        h, p = pairs[used[0]]
        used[0] += 1
        return wc(h, 2 * p + parity, 2 + 4 * side)

    def edge(h, s, t):
        kids.setdefault((s, h), []).append(t)

    lh = {}
    free = {}

    if cfg["C_a"] == "four":
        free[(C[0], 0)] = [-1, -2]
        free[(C[0], 1)] = [-1, -2]

    def helper(X, h, s):
        key = (X[0], h if names[X] in cfg["lh_half"] else 100 + h // 2)
        if key not in lh:
            side = (s % 8) // 4
            lst = free.setdefault((X[0], side), [1, -1, -2])
            if not lst:
                lst = free.setdefault((X[0], 1 - side), [1, -1, -2])
                side = 1 - side
            lh[key] = X[side] + lst.pop(0)
        return lh[key]

    def deliver(h, s, X, pol):
        if pol == "DD":
            edge(h, s, X[0])
            edge(h, s, X[1])
            return None
        if pol == "LH":
            r = helper(X, h, s)
            edge(h, s, r)
            edge(h, r, X[0])
            edge(h, r, X[1])
            return r
        f = (h % 2) if pol == "SDh" else int(pol[2])
        edge(h, s, X[f])
        edge(h, X[f], X[1 - f])
        return X[f]

    def pol1(i, X):
        return {"h": "SDh", "LH": "LH", "DD": "DD"}.get(cfg["hop1"][names[X]], "SD%d" % i)

    def polr(pol, side):
        return ("SD%d" % side) if pol == "SD" else pol

    for i in (0, 1):
        for k in (0, 1):
            h = 2 * i + k
            edge(h, A[i], A[1 - i])
            if cfg["C_a"] == "four":
                f = C[i] + (1 if k != i else 0)
                edge(h, A[i], f)
                for t in (D[0], D[1], C[0], C[1]):
                    if t != f:
                        edge(h, f, t)
            else:
                f = deliver(h, A[i], C, pol1(i, C))
                deliver(h, f, D, polr(cfg["D_a"], (f % 8) // 4))
            sd = cfg["B_a_side"][i][k]
            r = relay(0, sd)
            edge(h, A[i], r)
            deliver(h, r, B, polr(cfg["B_a"], sd))
            h = 4 + 2 * i + k
            edge(h, B[i], B[1 - i])
            sd = cfg["b_side"][i][k]
            r = relay(1, sd)
            edge(h, B[i], r)
            deliver(h, r, A, polr(cfg["A_b"], sd))
            deliver(h, r, C, polr(cfg["C_b"], sd))
            if i == 0:
                deliver(h, B[0], D, pol1(0, D))
            else:
                kind, pol = cfg["D_b1"]
                if kind == "peer":
                    deliver(h, B[0], D, polr(pol, 0))
                elif kind == "help":
                    edge(h, B[1], B[0] + 1)
                    deliver(h, B[0] + 1, D, polr(pol, 0))
                else:
                    deliver(h, r, D, polr(pol, 0))
            for (X, O, base, key) in ((C, D, 8, "B_c1"), (D, C, 12, "B_d1")):
                h = base + 2 * i + k
                edge(h, X[i], X[1 - i])
                deliver(h, X[i], A, pol1(i, A))
                if i == 1 and cfg[key][0] == "via":
                    r = helper(D, 14, D[0])
                    edge(h, X[1], r)
                    edge(h, r, D[0])
                    edge(h, r, D[1])
                    deliver(h, r, B, polr(cfg[key][1], 0))
                    continue
                deliver(h, X[i], O, pol1(i, O))
                if i == 0:
                    deliver(h, X[0], B, pol1(0, B))
                else:
                    kind, pol = cfg[key]
                    if kind == "peer":
                        deliver(h, X[0], B, polr(pol, 0))
                    elif kind == "help":
                        r = X[0] + 1 if X is C else helper(X, h, X[0])
                        edge(h, X[1], r)
                        deliver(h, r, B, polr(pol, 0))
                    else:
                        r = relay(0, 1)
                        edge(h, X[1], r)
                        deliver(h, r, B, polr(pol, 1))

    est = {}

    def walk(h, s, t0):
        for t in kids.get((s, h), []):
            est[(t, h)] = t0 + (1.0 if t // 8 == s // 8 else 1.5)
            walk(h, t, est[(t, h)])

    for h in range(16):
        est[(cores[h // 2], h)] = 0.0
        walk(h, cores[h // 2], 0.0)

    def height(t, h):
        return max([0.0] + [(1.0 if u // 8 == t // 8 else 1.5) + height(u, h) for u in kids.get((t, h), [])])

    cnt = {}

    def alloc(s, tasks):
        off, on, trs = [], [], []
        for (h, ds0) in tasks:
            ds = sorted(ds0, key=lambda t: -height(t, h)) if cfg["order"] else ds0
            o = [t for t in ds if t // 8 != s // 8]
            n = [t for t in ds if t // 8 == s // 8]
            if o:
                off.append((h, o))
            if n:
                on.append((h, n))

        def place(lst, base, width):
            n = 1
            while n < len(lst):
                n *= 2
            e = width // n
            for q, (h, ds) in enumerate(lst):
                trs.append((h, ds, ((1 << e) - 1) << (base + q * e), e))
                for t in ds:
                    cnt[(t, h)] = e

        if off and on:
            place(off, 0, 8)
            place(on, 8, 8)
        elif off:
            place(off, 0, 8)
        else:
            place(on, 0, 16)
        return trs

    senders = sorted(set(s for (s, h) in kids))
    calls = {}
    for s in senders:
        groups = {}
        for (s2, h) in sorted(kids):
            if s2 == s:
                e = est[(s, h)]
                if e == 0.0 and cfg["split"]:
                    urgent = [t for t in kids[(s, h)] if height(t, h) >= cfg["split"]]
                    late = [t for t in kids[(s, h)] if t not in urgent]
                    if urgent:
                        groups.setdefault((e, 0), []).append((h, urgent))
                    if late:
                        groups.setdefault((e, 1), []).append((h, late))
                elif cfg["merge"] == "all" and e >= 2.5:
                    groups.setdefault((9.0, 0), []).append((h, kids[(s, h)]))
                else:
                    groups.setdefault((e, 0 if (cfg["merge"] or e == 0.0) else h // 2), []).append((h, kids[(s, h)]))
        calls[s] = [(key, sorted(set(h for (h, _d) in groups[key])), alloc(s, groups[key])) for key in sorted(groups)]

    prog = {}
    for s in senders:
        gq, sy, sc = [], [], []
        total = 0
        n0 = 0
        rank = cores.index(s) if s in cores else None
        for (key, hs, trs) in calls[s]:
            n = sum(e for (_h, _d, _m, e) in trs)
            if key[0] == 0.0:
                if not sy:
                    sy.append(("load", rank))
                    gq.append(("wait", "ld", 16))
                gq.append(("send", trs, "sn0"))
                n0 += n
            else:
                for h in hs:
                    gq.append(("wait", "p%d" % h, cnt[(s, h)]))
                gq.append(("send", trs, "snt"))
                total += n
        if rank is not None:
            if cfg["own"] == "sent":
                sc.append(("wait", "sn0", n0))
            else:
                gq.append(("wait", "sn0", n0))
                if cfg["own"] == "ld":
                    sc.append(("wait", "ld", 16))
            sc.append(("own", rank))
            items = []
            for j in range(8):
                if j == rank:
                    continue
                e0, e1 = est[(s, 2 * j)], est[(s, 2 * j + 1)]
                if e0 == e1:
                    items.append((e0, j, None))
                else:
                    items.append((e0, j, 0))
                    items.append((e1, j, 1))
            items.sort(key=lambda it: (it[0], it[1]))
            for q, (e, j, k) in enumerate(items):
                dq = sy if q % 2 == 0 else sc
                for h in ((2 * j, 2 * j + 1) if k is None else (2 * j + k,)):
                    dq.append(("wait", "p%d" % h, cnt[(s, h)]))
                dq.append(("store", j, k))
            if total:
                gq.append(("wait", "snt", total))
            gq.append(("wait", "st", 16 * (len(items) + 1)))
        else:
            gq.append(("wait", "snt", total))
        prog[s] = {"g": gq, "sync": sy, "scalar": sc}
    return prog


CACHE = {}


def rank_program(g, core, T, topo):
    if "p" not in CACHE:
        CACHE["p"] = build(list(T.cores), CFG)
    prog = CACHE["p"].get(core)
    if prog is None:
        return
    for name, q in (("sync", g.sync), ("scalar", g.scalar), ("g", g)):
        for op in prog[name]:
            if op[0] == "wait":
                q.wait_ge(T.sem[op[1]], op[2])
            elif op[0] == "load":
                r = op[1]
                q.dma_start(T.buf[2 * r:2 * r + 2], T.x[:]).then_inc(T.sem.ld, 16)
            elif op[0] == "own":
                r = op[1]
                q.dma_start(T.y[:, 256 * r:256 * r + 256], T.x[:]).then_inc(T.sem.st, 16)
            elif op[0] == "store":
                j, k = op[1], op[2]
                if k is None:
                    q.dma_start(T.y[:, 256 * j:256 * j + 256], T.buf[2 * j:2 * j + 2]).then_inc(T.sem.st, 16)
                else:
                    q.dma_start(T.y[64 * k:64 * k + 64, 256 * j:256 * j + 256], T.buf[2 * j + k]).then_inc(T.sem.st, 16)
            else:
                trs = []
                for (h, ds, mask, _e) in op[1]:
                    ids = []
                    for t in ds:
                        rid, pid = topo.addr(t, core)
                        ids.append(DstId(rid=rid, pnc=pid))
                    trs.append(RemoteDMATransfer(dst_ids=ids, dma_engine_mask=mask, remote_sem=T.sem["p%d" % h],
                                                 srcs=[T.buf[h]], dsts=[T.buf[h] for _t in ds]))
                q.remote_dma_fused(trs, local_sem=T.sem[op[2]])
